import numpy as np
import ml_dtypes


def mxq(x, axis, fmt="e4m3"):
    dtype, down = {"e4m3": (ml_dtypes.float8_e4m3fn, 7), "e5m2": (ml_dtypes.float8_e5m2, 14)}[fmt]
    v = np.moveaxis(np.asarray(x, np.float32).astype(ml_dtypes.bfloat16).astype(np.float64), axis, -1)
    blocks = v.reshape(v.shape[:-1] + (-1, 32))
    amax = np.abs(blocks).max(-1, keepdims=True)
    byte = np.maximum(np.where(amax > 0, np.frexp(amax)[1] - 1 + 127, 0) - down, 1)
    scale = np.exp2(byte - 127.0)
    codes = (blocks / scale).astype(np.float32).astype(dtype).astype(np.float64)
    return np.moveaxis((codes * scale).reshape(v.shape), -1, axis)


WIDE = False


def mx_kscale(k):
    if not WIDE:
        return np.ones(k)
    levels = np.array([10, -10, 5, -5, 0])
    if k % 512:
        return np.exp2(np.random.permutation(np.resize(levels, k // 32))).repeat(32)
    a = np.empty((k // 512, 16))
    for p in range(k // 512):
        a[p, :8] = np.random.permutation(np.resize(levels, 8))
        for g in range(8):
            far = levels[np.abs(levels - a[p, g]) >= 10]
            a[p, g + 8] = far[np.random.randint(len(far))]
    return np.exp2(a.ravel()).repeat(32)


def f64(x):
    return np.asarray(x).astype(np.float64)


E2M1 = np.array([0.0, 0.5, 1.0, 1.5, 2.0, 3.0, 4.0, 6.0, -0.0, -0.5, -1.0, -1.5, -2.0, -3.0, -4.0, -6.0])


def pack_weight(w, fmt):
    k, n = w.shape
    w = f64(np.asarray(w, np.float32).astype(ml_dtypes.bfloat16)).reshape(k // 32, 32, n)
    amax = np.abs(w).max(1)
    if fmt == "e4m3":
        byte = np.frexp(amax)[1] - 1 + 127 - 7
    else:
        mant, ex = np.frexp(amax / 6.0)
        byte = np.where(mant > 0.5, ex, ex - 1) + 127
    byte = np.clip(np.where(amax > 0, byte, 1), 1, 254)
    scaled = (w * np.exp2(127.0 - byte)[:, None, :]).reshape(k, n).astype(np.float32)
    by_word = np.ascontiguousarray(scaled.reshape(k // 512, 128, 4, n).transpose(0, 1, 3, 2))
    if fmt == "e4m3":
        words = by_word.astype(ml_dtypes.float8_e4m3fn).view(np.uint8)
    else:
        c = by_word.astype(ml_dtypes.float4_e2m1fn).view(np.uint8) & 0xF
        words = (c[..., 0::2] | (c[..., 1::2] << 4)).reshape(k // 512, 128, 2 * n)
    return np.ascontiguousarray(words), np.ascontiguousarray(byte.astype(np.uint8).reshape(k // 512, 16, n))


def unpack_weight(words, scales, fmt):
    g, _, n = scales.shape
    words = np.ascontiguousarray(words).reshape(g, 128, n, -1)
    if fmt == "e4m3":
        vals = words.view(ml_dtypes.float8_e4m3fn).astype(np.float64)
    else:
        nib = np.empty((g, 128, n, 4), np.uint8)
        nib[..., 0::2] = words & 0xF
        nib[..., 1::2] = words >> 4
        vals = E2M1[nib]
    vals = vals * np.repeat(np.exp2(scales.astype(np.float64) - 127.0), 8, axis=1)[..., None]
    return vals.transpose(0, 1, 3, 2).reshape(g * 512, n)


K, M, T = 512, 1024, 512


def setup_inputs():
    n = np.random.standard_normal
    s = mx_kscale(K)[:, None]
    p_wr = pack_weight(n((K, M)) / np.sqrt(K) / s, "e2m1")
    p_wk = pack_weight(n((K, M)) / np.sqrt(K) / s, "e4m3")
    return {
        "x": (np.round(32.0 * n((K, T + 1))) / 32.0 * s).astype(np.float32),
        "mu": (np.random.randint(1, 16, (K, 3)) / 16.0).astype(np.float32),
        "wr_words": p_wr[0],
        "wr_scales": p_wr[1],
        "wk_words": p_wk[0],
        "wk_scales": p_wk[1],
        "wv": (n((K, M)) / np.sqrt(K) / s).astype(np.float32),
    }


def reference(x, mu, wr_words, wr_scales, wk_words, wk_scales, wv):
    now, before = f64(x)[:, 1:], f64(x)[:, :-1]
    xr_, xk_, xv_ = [mxq(now + f64(mu)[:, i:i + 1] * (before - now), 0, "e4m3") for i in range(3)]
    wr_ = unpack_weight(wr_words, wr_scales, "e2m1")
    wk_ = unpack_weight(wk_words, wk_scales, "e4m3")
    wv_ = mxq(f64(wv), 0, "e4m3")
    return xr_.T @ wr_, xk_.T @ wk_, xv_.T @ wv_

@@ -1,0 +1,188 @@
+from contextlib import ExitStack
+
+import concourse.mybir as mybir
+
+K, M, T = 512, 1024, 512
+FLOPS = 3 * 2 * K * M * T
+
+F32 = mybir.dt.float32
+BF16 = mybir.dt.bfloat16
+I32 = mybir.dt.int32
+U32 = mybir.dt.uint32
+U8 = mybir.dt.uint8
+FP8X4 = mybir.dt.float8_e4m3fn_x4
+FP4X4 = mybir.dt.float4_e2m1fn_x4
+ALU = mybir.AluOpType
+ACT = mybir.ActivationFunctionType
+
+P = 128
+PACK = 4
+N_TILE = 512
+HALF = T // 2
+X_PAD = 3
+X_ROW = 520
+RUN = 4
+
+
+def by_runs(rows):
+    return rows.rearrange("p j (c i) -> p c j i", i=RUN)
+
+
+def words_by_runs(words):
+    return words.rearrange("p (c i) j -> p c j i", i=RUN)
+
+
+def tile_mix_rwkv_tm_none_kernel(tc, x, mu, wr_words, wr_scales, wk_words, wk_scales, wv, out_0, out_1, out_2):
+    nc = tc.nc
+    with ExitStack() as ctx:
+        keep = ctx.enter_context(tc.tile_pool(name="keep", bufs=1))
+        results = ctx.enter_context(tc.tile_pool(name="results", bufs=12))
+        psum = ctx.enter_context(tc.psum_pool(name="psum", bufs=8))
+        ctx.enter_context(tc.manual_schedule())
+
+        x_sb = keep.tile([P, PACK, X_ROW], F32, align_bytes=64)
+        mu_sb = keep.tile([P, PACK * 3], F32, align_bytes=64)
+        wr_sb = keep.tile([P, 2 * M], U8, align_bytes=64)
+        wk_sb = keep.tile([P, M], U32, align_bytes=64)
+        w_planes = keep.tile([P, 2 * M], U8, align_bytes=64)
+        wv_a = keep.tile([P, PACK, 256], F32, align_bytes=64)
+        wv_b = keep.tile([P, PACK, M - 256], F32, align_bytes=64)
+        warm = keep.tile([P, 2], F32, align_bytes=64)
+        diff = keep.tile([P, PACK, T], F32, align_bytes=64)
+        step_r = keep.tile([P, PACK, T], F32, align_bytes=64)
+        blend_k = keep.tile([P, PACK, T], F32, align_bytes=64)
+        blend_v = keep.tile([P, PACK, T], F32, align_bytes=64)
+        x16 = [keep.tile([P, T, PACK], BF16, align_bytes=64, name="x16_%d" % i) for i in range(3)]
+        x_codes = [keep.tile([P, T], U32, align_bytes=64, name="x_codes_%d" % i) for i in range(3)]
+        x_scales = [keep.tile([P, T], U8, align_bytes=64, name="x_scales_%d" % i) for i in range(3)]
+        wv16 = keep.tile([P, M, PACK], BF16, align_bytes=64)
+        wv_codes = keep.tile([P, M], U32, align_bytes=64)
+        wv_scales = keep.tile([P, M], U8, align_bytes=64)
+
+        nc.gpsimd.memset(warm[:, 0:1], 0.0)
+        nc.vector.memset(w_planes[:].bitcast(I32), 0)
+        nc.scalar.dma_start(out=mu_sb[:], in_=mu.rearrange("(p j) c -> p (j c)", j=PACK))
+        x_rows = x.rearrange("(p j) t -> p j t", j=PACK)
+        for j in range(PACK):
+            nc.sync.dma_start(out=x_sb[:, j, X_PAD:X_PAD + T + 1], in_=x_rows[:, j, :])
+
+        def load_plane(queue, which, scales):
+            for r in range(4):
+                queue.dma_start(out=w_planes[r:P:32, which * M:(which + 1) * M].bitcast(I32),
+                                in_=scales[0, r:16:4, :].bitcast(I32))
+
+        wv_rows = wv.rearrange("(p j) n -> p j n", j=PACK)
+        nc.scalar.activation(out=warm[:, 1:2], in_=warm[:, 0:1], func=ACT.Copy)
+        nc.sync.dma_start(out=wv_a[:], in_=wv_rows[:, :, 0:256])
+        load_plane(nc.sync, 0, wr_scales)
+        nc.sync.dma_start(out=wr_sb[:].bitcast(I32), in_=wr_words[0].bitcast(I32))
+        nc.sync.dma_start(out=wk_sb[:].bitcast(I32), in_=wk_words[0].rearrange("p n i -> p (n i)").bitcast(I32))
+        load_plane(nc.sync, 1, wk_scales)
+        nc.sync.dma_start(out=wv_b[:], in_=wv_rows[:, :, 256:M])
+
+        before = x_sb[:, :, X_PAD:X_PAD + T]
+        now = x_sb[:, :, X_PAD + 1:X_PAD + 1 + T]
+
+        def mu_col(j, proj):
+            return mu_sb[:, 3 * j + proj:3 * j + proj + 1]
+
+        def halves(h):
+            return slice(h * HALF, (h + 1) * HALF)
+
+        def blend_row(dst, j, proj):
+            nc.vector.scalar_tensor_tensor(out=dst[:, j, :], in0=diff[:, j, :], scalar=mu_col(j, proj),
+                                           in1=now[:, j, :], op0=ALU.mult, op1=ALU.add)
+
+        def add_step_r(tt):
+            cols = slice(tt * P, (tt + 1) * P)
+            nc.vector.tensor_tensor(out=words_by_runs(x16[0][:, cols, :]), in0=by_runs(step_r[:, :, cols]),
+                                    in1=by_runs(now[:, :, cols]), op=ALU.add)
+
+        def quantize_r(cols):
+            quantize(x_codes[0], x_scales[0], x16[0], cols)
+
+        def cast_wv(copy, quarter):
+            src = wv_a[:] if quarter == 0 else wv_b[:, :, (quarter - 1) * 256:quarter * 256]
+            copy(out=words_by_runs(wv16[:, quarter * 256:(quarter + 1) * 256, :]), in_=by_runs(src))
+
+        def interleave_x(src, proj, h):
+            nc.vector.tensor_copy(out=words_by_runs(x16[proj][:, halves(h), :]), in_=by_runs(src[:, :, halves(h)]))
+
+        def quantize(codes, scales, src16, cols):
+            nc.vector.quantize_mx(out=codes[:, cols].bitcast(FP8X4), scales=scales[:, cols],
+                                  in_=src16[:, cols, :].rearrange("p c j -> p (c j)"))
+
+        def quantize_x(proj, h):
+            quantize(x_codes[proj], x_scales[proj], x16[proj], halves(h))
+
+        def weights(proj, nh):
+            cols = slice(nh * N_TILE, (nh + 1) * N_TILE)
+            if proj == 0:
+                return wr_sb[:, 2 * cols.start:2 * cols.stop].bitcast(FP4X4), w_planes[:, cols]
+            if proj == 1:
+                return wk_sb[:, cols].bitcast(FP8X4), w_planes[:, M + cols.start:M + cols.stop]
+            return wv_codes[:, cols].bitcast(FP8X4), wv_scales[:, cols]
+
+        def product(proj, tt, nh, dst, copy):
+            tokens = slice(tt * P, (tt + 1) * P)
+            rhs, rhs_scale = weights(proj, nh)
+            acc = psum.tile([P, N_TILE], F32, name="acc")
+            nc.tensor.matmul_mx(out=acc[:], lhsT=x_codes[proj][:, tokens].bitcast(FP8X4), lhsT_scale=x_scales[proj][:, tokens],
+                                rhs=rhs, rhs_scale=rhs_scale, start=True, stop=True)
+            copy(out=dst, in_=acc[:])
+
+        def full_rows(proj, out, tt):
+            res = results.tile([P, 2, N_TILE], F32, name="res")
+            for nh in range(2):
+                product(proj, tt, nh, res[:, nh, :], nc.scalar.copy)
+            nc.sync.dma_start(out=out[tt * P:(tt + 1) * P, :], in_=res[:].rearrange("p a n -> p (a n)"))
+
+        def half_rows_v(h, nh, copies):
+            res = results.tile([P, 2, N_TILE], F32, name="res")
+            for a in range(2):
+                product(2, 2 * h + a, nh, res[:, a, :], copies[a])
+            nc.sync.dma_start(out=out_2[halves(h), nh * N_TILE:(nh + 1) * N_TILE].rearrange("(a p) n -> p a n", p=P), in_=res[:])
+
+        for j in range(PACK):
+            last = j == PACK - 1
+            for cols in [halves(0), halves(1)] if last else [slice(0, T)]:
+                nc.vector.tensor_tensor(out=diff[:, j, cols], in0=before[:, j, cols], in1=now[:, j, cols], op=ALU.subtract)
+            for cols in [slice(0, P), slice(P, HALF), halves(1)] if last else [slice(0, T)]:
+                nc.scalar.activation(out=step_r[:, j, cols], in_=diff[:, j, cols], func=ACT.Copy, scale=mu_col(j, 0))
+        cast_wv(nc.scalar.copy, 0)
+
+        add_step_r(0)
+        add_step_r(1)
+        quantize_r(slice(0, P))
+        add_step_r(2)
+        quantize_r(slice(P, HALF))
+        add_step_r(3)
+        blend_row(blend_k, 0, 1)
+        quantize_r(halves(1))
+        for tt in range(4):
+            full_rows(0, out_0, tt)
+        cast_wv(nc.scalar.copy, 1)
+        for j in range(1, PACK):
+            blend_row(blend_k, j, 1)
+        blend_row(blend_v, 0, 2)
+        interleave_x(blend_k, 1, 0)
+        interleave_x(blend_k, 1, 1)
+        quantize_x(1, 0)
+        blend_row(blend_v, 1, 2)
+        quantize_x(1, 1)
+        for tt in range(4):
+            full_rows(1, out_1, tt)
+        for j in range(2, PACK):
+            blend_row(blend_v, j, 2)
+        quantize(wv_codes, wv_scales, wv16, slice(0, N_TILE))
+        interleave_x(blend_v, 2, 0)
+        interleave_x(blend_v, 2, 1)
+        quantize_x(2, 0)
+        cast_wv(nc.vector.tensor_copy, 2)
+        cast_wv(nc.vector.tensor_copy, 3)
+        quantize_x(2, 1)
+        quantize(wv_codes, wv_scales, wv16, slice(N_TILE, M))
+        half_rows_v(0, 0, [nc.scalar.copy, nc.scalar.copy])
+        half_rows_v(1, 0, [nc.scalar.copy, nc.scalar.copy])
+        half_rows_v(0, 1, [nc.vector.tensor_copy, nc.vector.tensor_copy])
+        half_rows_v(1, 1, [nc.scalar.copy, nc.vector.tensor_copy])

@@ -44,13 +44,12 @@ def tile_mix_rwkv_tm_none_kernel(tc, x, mu, wr_words, wr_scales, wk_words, wk_sc
         mu_sb = keep.tile([P, PACK * 3], F32, align_bytes=64)
         wr_sb = keep.tile([P, 2 * M], U8, align_bytes=64)
         wk_sb = keep.tile([P, M], U32, align_bytes=64)
-        w_planes = keep.tile([P, 2 * M], U8, align_bytes=64)
-        wv_a = keep.tile([P, PACK, 256], F32, align_bytes=64)
-        wv_b = keep.tile([P, PACK, M - 256], F32, align_bytes=64)
+        w_planes = [keep.tile([P, M], U8, align_bytes=64, name="w_plane_%d" % i) for i in range(2)]
+        wv_sb = keep.tile([P, PACK, M], F32, align_bytes=64)
         warm = keep.tile([P, 2], F32, align_bytes=64)
         diff = keep.tile([P, PACK, T], F32, align_bytes=64)
         step_r = keep.tile([P, PACK, T], F32, align_bytes=64)
-        blend_k = keep.tile([P, PACK, T], F32, align_bytes=64)
+        step_k = keep.tile([P, PACK, T], F32, align_bytes=64)
         blend_v = keep.tile([P, PACK, T], F32, align_bytes=64)
         x16 = [keep.tile([P, T, PACK], BF16, align_bytes=64, name="x16_%d" % i) for i in range(3)]
         x_codes = [keep.tile([P, T], U32, align_bytes=64, name="x_codes_%d" % i) for i in range(3)]
@@ -59,8 +58,9 @@ def tile_mix_rwkv_tm_none_kernel(tc, x, mu, wr_words, wr_scales, wk_words, wk_sc
         wv_codes = keep.tile([P, M], U32, align_bytes=64)
         wv_scales = keep.tile([P, M], U8, align_bytes=64)
 
-        nc.gpsimd.memset(warm[:, 0:1], 0.0)
-        nc.vector.memset(w_planes[:].bitcast(I32), 0)
+        nc.vector.memset(warm[:, 0:1], 0.0)
+        nc.vector.memset(w_planes[0][:].bitcast(I32), 0)
+        nc.vector.memset(w_planes[1][:].bitcast(I32), 0)
         nc.scalar.dma_start(out=mu_sb[:], in_=mu.rearrange("(p j) c -> p (j c)", j=PACK))
         x_rows = x.rearrange("(p j) t -> p j t", j=PACK)
         for j in range(PACK):
@@ -68,17 +68,16 @@ def tile_mix_rwkv_tm_none_kernel(tc, x, mu, wr_words, wr_scales, wk_words, wk_sc
 
         def load_plane(queue, which, scales):
             for r in range(4):
-                queue.dma_start(out=w_planes[r:P:32, which * M:(which + 1) * M].bitcast(I32),
+                queue.dma_start(out=w_planes[which][r:P:32, :].bitcast(I32),
                                 in_=scales[0, r:16:4, :].bitcast(I32))
 
         wv_rows = wv.rearrange("(p j) n -> p j n", j=PACK)
         nc.scalar.activation(out=warm[:, 1:2], in_=warm[:, 0:1], func=ACT.Copy)
-        nc.sync.dma_start(out=wv_a[:], in_=wv_rows[:, :, 0:256])
-        load_plane(nc.sync, 0, wr_scales)
         nc.sync.dma_start(out=wr_sb[:].bitcast(I32), in_=wr_words[0].bitcast(I32))
+        load_plane(nc.sync, 0, wr_scales)
         nc.sync.dma_start(out=wk_sb[:].bitcast(I32), in_=wk_words[0].rearrange("p n i -> p (n i)").bitcast(I32))
+        nc.sync.dma_start(out=wv_sb[:], in_=wv_rows)
         load_plane(nc.sync, 1, wk_scales)
-        nc.sync.dma_start(out=wv_b[:], in_=wv_rows[:, :, 256:M])
 
         before = x_sb[:, :, X_PAD:X_PAD + T]
         now = x_sb[:, :, X_PAD + 1:X_PAD + 1 + T]
@@ -93,34 +92,33 @@ def tile_mix_rwkv_tm_none_kernel(tc, x, mu, wr_words, wr_scales, wk_words, wk_sc
             nc.vector.scalar_tensor_tensor(out=dst[:, j, :], in0=diff[:, j, :], scalar=mu_col(j, proj),
                                            in1=now[:, j, :], op0=ALU.mult, op1=ALU.add)
 
-        def add_step_r(tt):
-            cols = slice(tt * P, (tt + 1) * P)
-            nc.vector.tensor_tensor(out=words_by_runs(x16[0][:, cols, :]), in0=by_runs(step_r[:, :, cols]),
+        def tile_cols(tt):
+            return slice(tt * P, (tt + 1) * P)
+
+        def add_step(proj, step, cols):
+            nc.vector.tensor_tensor(out=words_by_runs(x16[proj][:, cols, :]), in0=by_runs(step[:, :, cols]),
                                     in1=by_runs(now[:, :, cols]), op=ALU.add)
 
-        def quantize_r(cols):
-            quantize(x_codes[0], x_scales[0], x16[0], cols)
-
         def cast_wv(copy, quarter):
-            src = wv_a[:] if quarter == 0 else wv_b[:, :, (quarter - 1) * 256:quarter * 256]
+            src = wv_sb[:, :, quarter * 256:(quarter + 1) * 256]
             copy(out=words_by_runs(wv16[:, quarter * 256:(quarter + 1) * 256, :]), in_=by_runs(src))
 
-        def interleave_x(src, proj, h):
-            nc.vector.tensor_copy(out=words_by_runs(x16[proj][:, halves(h), :]), in_=by_runs(src[:, :, halves(h)]))
+        def interleave_v(cols):
+            nc.vector.tensor_copy(out=words_by_runs(x16[2][:, cols, :]), in_=by_runs(blend_v[:, :, cols]))
 
         def quantize(codes, scales, src16, cols):
             nc.vector.quantize_mx(out=codes[:, cols].bitcast(FP8X4), scales=scales[:, cols],
                                   in_=src16[:, cols, :].rearrange("p c j -> p (c j)"))
 
-        def quantize_x(proj, h):
-            quantize(x_codes[proj], x_scales[proj], x16[proj], halves(h))
+        def quantize_x(proj, cols):
+            quantize(x_codes[proj], x_scales[proj], x16[proj], cols)
 
         def weights(proj, nh):
             cols = slice(nh * N_TILE, (nh + 1) * N_TILE)
             if proj == 0:
-                return wr_sb[:, 2 * cols.start:2 * cols.stop].bitcast(FP4X4), w_planes[:, cols]
+                return wr_sb[:, 2 * cols.start:2 * cols.stop].bitcast(FP4X4), w_planes[0][:, cols]
             if proj == 1:
-                return wk_sb[:, cols].bitcast(FP8X4), w_planes[:, M + cols.start:M + cols.stop]
+                return wk_sb[:, cols].bitcast(FP8X4), w_planes[1][:, cols]
             return wv_codes[:, cols].bitcast(FP8X4), wv_scales[:, cols]
 
         def product(proj, tt, nh, dst, copy):
@@ -131,17 +129,11 @@ def tile_mix_rwkv_tm_none_kernel(tc, x, mu, wr_words, wr_scales, wk_words, wk_sc
                                 rhs=rhs, rhs_scale=rhs_scale, start=True, stop=True)
             copy(out=dst, in_=acc[:])
 
-        def full_rows(proj, out, tt):
+        def full_rows(proj, out, tt, copies):
             res = results.tile([P, 2, N_TILE], F32, name="res")
             for nh in range(2):
-                product(proj, tt, nh, res[:, nh, :], nc.scalar.copy)
+                product(proj, tt, nh, res[:, nh, :], copies[nh])
             nc.sync.dma_start(out=out[tt * P:(tt + 1) * P, :], in_=res[:].rearrange("p a n -> p (a n)"))
-
-        def half_rows_v(h, nh, copies):
-            res = results.tile([P, 2, N_TILE], F32, name="res")
-            for a in range(2):
-                product(2, 2 * h + a, nh, res[:, a, :], copies[a])
-            nc.sync.dma_start(out=out_2[halves(h), nh * N_TILE:(nh + 1) * N_TILE].rearrange("(a p) n -> p a n", p=P), in_=res[:])
 
         for j in range(PACK):
             last = j == PACK - 1
@@ -149,40 +141,39 @@ def tile_mix_rwkv_tm_none_kernel(tc, x, mu, wr_words, wr_scales, wk_words, wk_sc
                 nc.vector.tensor_tensor(out=diff[:, j, cols], in0=before[:, j, cols], in1=now[:, j, cols], op=ALU.subtract)
             for cols in [slice(0, P), slice(P, HALF), halves(1)] if last else [slice(0, T)]:
                 nc.scalar.activation(out=step_r[:, j, cols], in_=diff[:, j, cols], func=ACT.Copy, scale=mu_col(j, 0))
-        cast_wv(nc.scalar.copy, 0)
+        for j in range(PACK):
+            nc.scalar.activation(out=step_k[:, j, :], in_=diff[:, j, :], func=ACT.Copy, scale=mu_col(j, 1))
+        scalar_only = [nc.scalar.copy, nc.scalar.copy]
+        both = [nc.scalar.copy, nc.vector.tensor_copy]
 
-        add_step_r(0)
-        add_step_r(1)
-        quantize_r(slice(0, P))
-        add_step_r(2)
-        quantize_r(slice(P, HALF))
-        add_step_r(3)
-        blend_row(blend_k, 0, 1)
-        quantize_r(halves(1))
-        for tt in range(4):
-            full_rows(0, out_0, tt)
-        cast_wv(nc.scalar.copy, 1)
-        for j in range(1, PACK):
-            blend_row(blend_k, j, 1)
+        add_step(0, step_r, tile_cols(0))
+        add_step(0, step_r, tile_cols(1))
+        quantize_x(0, tile_cols(0))
+        add_step(0, step_r, tile_cols(2))
+        quantize_x(0, tile_cols(1))
+        add_step(0, step_r, tile_cols(3))
         blend_row(blend_v, 0, 2)
-        interleave_x(blend_k, 1, 0)
-        interleave_x(blend_k, 1, 1)
-        quantize_x(1, 0)
-        blend_row(blend_v, 1, 2)
-        quantize_x(1, 1)
+        quantize_x(0, halves(1))
         for tt in range(4):
-            full_rows(1, out_1, tt)
-        for j in range(2, PACK):
-            blend_row(blend_v, j, 2)
-        quantize(wv_codes, wv_scales, wv16, slice(0, N_TILE))
-        interleave_x(blend_v, 2, 0)
-        interleave_x(blend_v, 2, 1)
-        quantize_x(2, 0)
-        cast_wv(nc.vector.tensor_copy, 2)
-        cast_wv(nc.vector.tensor_copy, 3)
-        quantize_x(2, 1)
-        quantize(wv_codes, wv_scales, wv16, slice(N_TILE, M))
-        half_rows_v(0, 0, [nc.scalar.copy, nc.scalar.copy])
-        half_rows_v(1, 0, [nc.scalar.copy, nc.scalar.copy])
-        half_rows_v(0, 1, [nc.vector.tensor_copy, nc.vector.tensor_copy])
-        half_rows_v(1, 1, [nc.scalar.copy, nc.vector.tensor_copy])
+            full_rows(0, out_0, tt, scalar_only)
+        cast_wv(nc.scalar.copy, 0)
+        add_step(1, step_k, halves(0))
+        add_step(1, step_k, halves(1))
+        quantize_x(1, halves(0))
+        blend_row(blend_v, 1, 2)
+        quantize_x(1, halves(1))
+        for tt in range(4):
+            full_rows(1, out_1, tt, scalar_only)
+        for quarter in range(1, 4):
+            cast_wv(nc.vector.tensor_copy, quarter)
+        blend_row(blend_v, 2, 2)
+        blend_row(blend_v, 3, 2)
+        quantize(wv_codes, wv_scales, wv16, slice(0, M))
+        interleave_v(tile_cols(0))
+        interleave_v(tile_cols(1))
+        quantize_x(2, tile_cols(0))
+        interleave_v(halves(1))
+        quantize_x(2, tile_cols(1))
+        quantize_x(2, halves(1))
+        for tt in range(4):
+            full_rows(2, out_2, tt, both)

@@ -21,7 +21,8 @@ N_TILE = 512
 HALF = T // 2
 X_PAD = 3
 X_ROW = 520
-RUN = 4
+RUN = 2
+PLANE_ROW = (0, 4)
 
 
 def by_runs(rows):
@@ -68,7 +69,7 @@ def tile_mix_rwkv_tm_none_kernel(tc, x, mu, wr_words, wr_scales, wk_words, wk_sc
 
         def load_plane(queue, which, scales):
             for r in range(4):
-                queue.dma_start(out=w_planes[which][r:P:32, :].bitcast(I32),
+                queue.dma_start(out=w_planes[which][PLANE_ROW[which] + r:P:32, :].bitcast(I32),
                                 in_=scales[0, r:16:4, :].bitcast(I32))
 
         wv_rows = wv.rearrange("(p j) n -> p j n", j=PACK)
@@ -88,9 +89,9 @@ def tile_mix_rwkv_tm_none_kernel(tc, x, mu, wr_words, wr_scales, wk_words, wk_sc
         def halves(h):
             return slice(h * HALF, (h + 1) * HALF)
 
-        def blend_row(dst, j, proj):
-            nc.vector.scalar_tensor_tensor(out=dst[:, j, :], in0=diff[:, j, :], scalar=mu_col(j, proj),
-                                           in1=now[:, j, :], op0=ALU.mult, op1=ALU.add)
+        def blend_v_row(j, h):
+            nc.vector.scalar_tensor_tensor(out=blend_v[:, j, halves(h)], in0=diff[:, j, halves(h)], scalar=mu_col(j, 2),
+                                           in1=now[:, j, halves(h)], op0=ALU.mult, op1=ALU.add)
 
         def tile_cols(tt):
             return slice(tt * P, (tt + 1) * P)
@@ -98,10 +99,6 @@ def tile_mix_rwkv_tm_none_kernel(tc, x, mu, wr_words, wr_scales, wk_words, wk_sc
         def add_step(proj, step, cols):
             nc.vector.tensor_tensor(out=words_by_runs(x16[proj][:, cols, :]), in0=by_runs(step[:, :, cols]),
                                     in1=by_runs(now[:, :, cols]), op=ALU.add)
-
-        def cast_wv(copy, quarter):
-            src = wv_sb[:, :, quarter * 256:(quarter + 1) * 256]
-            copy(out=words_by_runs(wv16[:, quarter * 256:(quarter + 1) * 256, :]), in_=by_runs(src))
 
         def interleave_v(cols):
             nc.vector.tensor_copy(out=words_by_runs(x16[2][:, cols, :]), in_=by_runs(blend_v[:, :, cols]))
@@ -118,7 +115,7 @@ def tile_mix_rwkv_tm_none_kernel(tc, x, mu, wr_words, wr_scales, wk_words, wk_sc
             if proj == 0:
                 return wr_sb[:, 2 * cols.start:2 * cols.stop].bitcast(FP4X4), w_planes[0][:, cols]
             if proj == 1:
-                return wk_sb[:, cols].bitcast(FP8X4), w_planes[1][:, cols]
+                return wk_sb[:, cols].bitcast(FP8X4), w_planes[1][PLANE_ROW[1]:P, cols]
             return wv_codes[:, cols].bitcast(FP8X4), wv_scales[:, cols]
 
         def product(proj, tt, nh, dst, copy):
@@ -144,7 +141,7 @@ def tile_mix_rwkv_tm_none_kernel(tc, x, mu, wr_words, wr_scales, wk_words, wk_sc
         for j in range(PACK):
             nc.scalar.activation(out=step_k[:, j, :], in_=diff[:, j, :], func=ACT.Copy, scale=mu_col(j, 1))
         scalar_only = [nc.scalar.copy, nc.scalar.copy]
-        both = [nc.scalar.copy, nc.vector.tensor_copy]
+        both = [nc.vector.tensor_copy, nc.scalar.copy]
 
         add_step(0, step_r, tile_cols(0))
         add_step(0, step_r, tile_cols(1))
@@ -152,28 +149,28 @@ def tile_mix_rwkv_tm_none_kernel(tc, x, mu, wr_words, wr_scales, wk_words, wk_sc
         add_step(0, step_r, tile_cols(2))
         quantize_x(0, tile_cols(1))
         add_step(0, step_r, tile_cols(3))
-        blend_row(blend_v, 0, 2)
+        blend_v_row(0, 0)
         quantize_x(0, halves(1))
         for tt in range(4):
             full_rows(0, out_0, tt, scalar_only)
-        cast_wv(nc.scalar.copy, 0)
         add_step(1, step_k, halves(0))
         add_step(1, step_k, halves(1))
         quantize_x(1, halves(0))
-        blend_row(blend_v, 1, 2)
+        blend_v_row(1, 0)
         quantize_x(1, halves(1))
         for tt in range(4):
             full_rows(1, out_1, tt, scalar_only)
-        for quarter in range(1, 4):
-            cast_wv(nc.vector.tensor_copy, quarter)
-        blend_row(blend_v, 2, 2)
-        blend_row(blend_v, 3, 2)
+        blend_v_row(2, 0)
+        blend_v_row(3, 0)
+        nc.vector.tensor_copy(out=words_by_runs(wv16[:]), in_=by_runs(wv_sb[:]))
+        interleave_v(halves(0))
         quantize(wv_codes, wv_scales, wv16, slice(0, M))
-        interleave_v(tile_cols(0))
-        interleave_v(tile_cols(1))
-        quantize_x(2, tile_cols(0))
-        interleave_v(halves(1))
-        quantize_x(2, tile_cols(1))
-        quantize_x(2, halves(1))
+        quantize_x(2, halves(0))
+        for j in range(PACK):
+            blend_v_row(j, 1)
+        interleave_v(tile_cols(2))
+        interleave_v(tile_cols(3))
+        quantize_x(2, tile_cols(2))
+        quantize_x(2, tile_cols(3))
         for tt in range(4):
-            full_rows(2, out_2, tt, both)
+            full_rows(2, out_2, tt, scalar_only if tt < 2 else both)

@@ -21,6 +21,7 @@ N_TILE = 512
 HALF = T // 2
 X_PAD = 3
 X_ROW = 520
+X_CUT = 264
 RUN = 2
 PLANE_ROW = (0, 4)
 
@@ -47,7 +48,7 @@ def tile_mix_rwkv_tm_none_kernel(tc, x, mu, wr_words, wr_scales, wk_words, wk_sc
         wk_sb = keep.tile([P, M], U32, align_bytes=64)
         w_planes = [keep.tile([P, M], U8, align_bytes=64, name="w_plane_%d" % i) for i in range(2)]
         wv_sb = keep.tile([P, PACK, M], F32, align_bytes=64)
-        warm = keep.tile([P, 2], F32, align_bytes=64)
+        mu_raw = keep.tile([P, PACK * 3], F32, align_bytes=64)
         diff = keep.tile([P, PACK, T], F32, align_bytes=64)
         step_r = keep.tile([P, PACK, T], F32, align_bytes=64)
         step_k = keep.tile([P, PACK, T], F32, align_bytes=64)
@@ -59,12 +60,13 @@ def tile_mix_rwkv_tm_none_kernel(tc, x, mu, wr_words, wr_scales, wk_words, wk_sc
         wv_codes = keep.tile([P, M], U32, align_bytes=64)
         wv_scales = keep.tile([P, M], U8, align_bytes=64)
 
-        nc.vector.memset(warm[:, 0:1], 0.0)
         nc.vector.memset(w_planes[0][:].bitcast(I32), 0)
         nc.vector.memset(w_planes[1][:].bitcast(I32), 0)
-        nc.scalar.dma_start(out=mu_sb[:], in_=mu.rearrange("(p j) c -> p (j c)", j=PACK))
+        nc.scalar.dma_start(out=mu_raw[:], in_=mu.rearrange("(p j) c -> p (j c)", j=PACK))
         x_rows = x.rearrange("(p j) t -> p j t", j=PACK)
-        for j in range(PACK):
+        nc.sync.dma_start(out=x_sb[:, 0, X_PAD:X_CUT], in_=x_rows[:, 0, 0:X_CUT - X_PAD])
+        nc.sync.dma_start(out=x_sb[:, 0, X_CUT:X_PAD + T + 1], in_=x_rows[:, 0, X_CUT - X_PAD:T + 1])
+        for j in range(1, PACK):
             nc.sync.dma_start(out=x_sb[:, j, X_PAD:X_PAD + T + 1], in_=x_rows[:, j, :])
 
         def load_plane(queue, which, scales):
@@ -73,10 +75,9 @@ def tile_mix_rwkv_tm_none_kernel(tc, x, mu, wr_words, wr_scales, wk_words, wk_sc
                                 in_=scales[0, r:16:4, :].bitcast(I32))
 
         wv_rows = wv.rearrange("(p j) n -> p j n", j=PACK)
-        nc.scalar.activation(out=warm[:, 1:2], in_=warm[:, 0:1], func=ACT.Copy)
         nc.sync.dma_start(out=wr_sb[:].bitcast(I32), in_=wr_words[0].bitcast(I32))
-        load_plane(nc.sync, 0, wr_scales)
         nc.sync.dma_start(out=wk_sb[:].bitcast(I32), in_=wk_words[0].rearrange("p n i -> p (n i)").bitcast(I32))
+        load_plane(nc.sync, 0, wr_scales)
         nc.sync.dma_start(out=wv_sb[:], in_=wv_rows)
         load_plane(nc.sync, 1, wk_scales)
 
@@ -132,41 +133,65 @@ def tile_mix_rwkv_tm_none_kernel(tc, x, mu, wr_words, wr_scales, wk_words, wk_sc
                 product(proj, tt, nh, res[:, nh, :], copies[nh])
             nc.sync.dma_start(out=out[tt * P:(tt + 1) * P, :], in_=res[:].rearrange("p a n -> p (a n)"))
 
-        for j in range(PACK):
-            last = j == PACK - 1
-            for cols in [halves(0), halves(1)] if last else [slice(0, T)]:
-                nc.vector.tensor_tensor(out=diff[:, j, cols], in0=before[:, j, cols], in1=now[:, j, cols], op=ALU.subtract)
-            for cols in [slice(0, P), slice(P, HALF), halves(1)] if last else [slice(0, T)]:
-                nc.scalar.activation(out=step_r[:, j, cols], in_=diff[:, j, cols], func=ACT.Copy, scale=mu_col(j, 0))
-        for j in range(PACK):
-            nc.scalar.activation(out=step_k[:, j, :], in_=diff[:, j, :], func=ACT.Copy, scale=mu_col(j, 1))
+        def subtract(j, cols):
+            nc.vector.tensor_tensor(out=diff[:, j, cols], in0=before[:, j, cols], in1=now[:, j, cols], op=ALU.subtract)
+
+        def scale_diff(step, proj, j, cols):
+            nc.scalar.activation(out=step[:, j, cols], in_=diff[:, j, cols], func=ACT.Copy, scale=mu_col(j, proj))
+
+        def cast_wv(nh):
+            cols = slice(nh * N_TILE, (nh + 1) * N_TILE)
+            nc.vector.tensor_copy(out=words_by_runs(wv16[:, cols, :]), in_=by_runs(wv_sb[:, :, cols]))
+
+        def quantize_wv(nh):
+            quantize(wv_codes, wv_scales, wv16, slice(nh * N_TILE, (nh + 1) * N_TILE))
+
+        every = slice(0, T)
         scalar_only = [nc.scalar.copy, nc.scalar.copy]
         both = [nc.vector.tensor_copy, nc.scalar.copy]
 
+        nc.vector.tensor_copy(out=mu_sb[:], in_=mu_raw[:])
+        for h in range(2):
+            subtract(0, halves(h))
+            scale_diff(step_r, 0, 0, halves(h))
+        scale_diff(step_k, 1, 0, every)
+        blend_v_row(0, 0)
+        for j in (1, 2):
+            subtract(j, every)
+            scale_diff(step_r, 0, j, every)
+        subtract(3, halves(0))
+        subtract(3, halves(1))
+        for cols in (tile_cols(0), tile_cols(1), halves(1)):
+            scale_diff(step_r, 0, 3, cols)
+        for j in range(1, PACK):
+            scale_diff(step_k, 1, j, every)
+
+        blend_v_row(1, 0)
         add_step(0, step_r, tile_cols(0))
         add_step(0, step_r, tile_cols(1))
         quantize_x(0, tile_cols(0))
         add_step(0, step_r, tile_cols(2))
         quantize_x(0, tile_cols(1))
         add_step(0, step_r, tile_cols(3))
-        blend_v_row(0, 0)
+        blend_v_row(2, 0)
         quantize_x(0, halves(1))
         for tt in range(4):
             full_rows(0, out_0, tt, scalar_only)
         add_step(1, step_k, halves(0))
         add_step(1, step_k, halves(1))
         quantize_x(1, halves(0))
-        blend_v_row(1, 0)
+        blend_v_row(3, 0)
         quantize_x(1, halves(1))
         for tt in range(4):
             full_rows(1, out_1, tt, scalar_only)
-        blend_v_row(2, 0)
-        blend_v_row(3, 0)
-        nc.vector.tensor_copy(out=words_by_runs(wv16[:]), in_=by_runs(wv_sb[:]))
+        cast_wv(0)
         interleave_v(halves(0))
-        quantize(wv_codes, wv_scales, wv16, slice(0, M))
+        quantize_wv(0)
         quantize_x(2, halves(0))
-        for j in range(PACK):
+        cast_wv(1)
+        blend_v_row(0, 1)
+        quantize_wv(1)
+        for j in range(1, PACK):
             blend_v_row(j, 1)
         interleave_v(tile_cols(2))
         interleave_v(tile_cols(3))

from contextlib import ExitStack

import concourse.mybir as mybir

K, M, T = 512, 1024, 512
FLOPS = 3 * 2 * K * M * T

F32 = mybir.dt.float32
BF16 = mybir.dt.bfloat16
I32 = mybir.dt.int32
U32 = mybir.dt.uint32
U8 = mybir.dt.uint8
FP8X4 = mybir.dt.float8_e4m3fn_x4
FP4X4 = mybir.dt.float4_e2m1fn_x4
ALU = mybir.AluOpType
ACT = mybir.ActivationFunctionType

P = 128
PACK = 4
N_TILE = 512
HALF = T // 2
X_PAD = 3
X_ROW = 520
X_CUT = 264
RUN = 2
PLANE_ROW = (0, 4)


def by_runs(rows):
    return rows.rearrange("p j (c i) -> p c j i", i=RUN)


def words_by_runs(words):
    return words.rearrange("p (c i) j -> p c j i", i=RUN)


def tile_mix_rwkv_tm_none_kernel(tc, x, mu, wr_words, wr_scales, wk_words, wk_scales, wv, out_0, out_1, out_2):
    nc = tc.nc
    with ExitStack() as ctx:
        keep = ctx.enter_context(tc.tile_pool(name="keep", bufs=1))
        results = ctx.enter_context(tc.tile_pool(name="results", bufs=12))
        psum = ctx.enter_context(tc.psum_pool(name="psum", bufs=8))
        ctx.enter_context(tc.manual_schedule())

        x_sb = keep.tile([P, PACK, X_ROW], F32, align_bytes=64)
        mu_sb = keep.tile([P, PACK * 3], F32, align_bytes=64)
        wr_sb = keep.tile([P, 2 * M], U8, align_bytes=64)
        wk_sb = keep.tile([P, M], U32, align_bytes=64)
        w_planes = [keep.tile([P, M], U8, align_bytes=64, name="w_plane_%d" % i) for i in range(2)]
        wv_sb = keep.tile([P, PACK, M], F32, align_bytes=64)
        mu_raw = keep.tile([P, PACK * 3], F32, align_bytes=64)
        diff = keep.tile([P, PACK, T], F32, align_bytes=64)
        step_r = keep.tile([P, PACK, T], F32, align_bytes=64)
        step_k = keep.tile([P, PACK, T], F32, align_bytes=64)
        blend_v = keep.tile([P, PACK, T], F32, align_bytes=64)
        x16 = [keep.tile([P, T, PACK], BF16, align_bytes=64, name="x16_%d" % i) for i in range(3)]
        x_codes = [keep.tile([P, T], U32, align_bytes=64, name="x_codes_%d" % i) for i in range(3)]
        x_scales = [keep.tile([P, T], U8, align_bytes=64, name="x_scales_%d" % i) for i in range(3)]
        wv16 = keep.tile([P, M, PACK], BF16, align_bytes=64)
        wv_codes = keep.tile([P, M], U32, align_bytes=64)
        wv_scales = keep.tile([P, M], U8, align_bytes=64)

        nc.vector.memset(w_planes[0][:].bitcast(I32), 0)
        nc.vector.memset(w_planes[1][:].bitcast(I32), 0)
        nc.scalar.dma_start(out=mu_raw[:], in_=mu.rearrange("(p j) c -> p (j c)", j=PACK))
        x_rows = x.rearrange("(p j) t -> p j t", j=PACK)
        nc.sync.dma_start(out=x_sb[:, 0, X_PAD:X_CUT], in_=x_rows[:, 0, 0:X_CUT - X_PAD])
        nc.sync.dma_start(out=x_sb[:, 0, X_CUT:X_PAD + T + 1], in_=x_rows[:, 0, X_CUT - X_PAD:T + 1])
        for j in range(1, PACK):
            nc.sync.dma_start(out=x_sb[:, j, X_PAD:X_PAD + T + 1], in_=x_rows[:, j, :])

        def load_plane(queue, which, scales):
            for r in range(4):
                queue.dma_start(out=w_planes[which][PLANE_ROW[which] + r:P:32, :].bitcast(I32),
                                in_=scales[0, r:16:4, :].bitcast(I32))

        wv_rows = wv.rearrange("(p j) n -> p j n", j=PACK)
        nc.sync.dma_start(out=wr_sb[:].bitcast(I32), in_=wr_words[0].bitcast(I32))
        nc.sync.dma_start(out=wk_sb[:].bitcast(I32), in_=wk_words[0].rearrange("p n i -> p (n i)").bitcast(I32))
        load_plane(nc.sync, 0, wr_scales)
        nc.sync.dma_start(out=wv_sb[:], in_=wv_rows)
        load_plane(nc.sync, 1, wk_scales)

        before = x_sb[:, :, X_PAD:X_PAD + T]
        now = x_sb[:, :, X_PAD + 1:X_PAD + 1 + T]

        def mu_col(j, proj):
            return mu_sb[:, 3 * j + proj:3 * j + proj + 1]

        def halves(h):
            return slice(h * HALF, (h + 1) * HALF)

        def blend_v_row(j, h):
            nc.vector.scalar_tensor_tensor(out=blend_v[:, j, halves(h)], in0=diff[:, j, halves(h)], scalar=mu_col(j, 2),
                                           in1=now[:, j, halves(h)], op0=ALU.mult, op1=ALU.add)

        def tile_cols(tt):
            return slice(tt * P, (tt + 1) * P)

        def add_step(proj, step, cols):
            nc.vector.tensor_tensor(out=words_by_runs(x16[proj][:, cols, :]), in0=by_runs(step[:, :, cols]),
                                    in1=by_runs(now[:, :, cols]), op=ALU.add)

        def interleave_v(cols):
            nc.vector.tensor_copy(out=words_by_runs(x16[2][:, cols, :]), in_=by_runs(blend_v[:, :, cols]))

        def quantize(codes, scales, src16, cols):
            nc.vector.quantize_mx(out=codes[:, cols].bitcast(FP8X4), scales=scales[:, cols],
                                  in_=src16[:, cols, :].rearrange("p c j -> p (c j)"))

        def quantize_x(proj, cols):
            quantize(x_codes[proj], x_scales[proj], x16[proj], cols)

        def weights(proj, nh):
            cols = slice(nh * N_TILE, (nh + 1) * N_TILE)
            if proj == 0:
                return wr_sb[:, 2 * cols.start:2 * cols.stop].bitcast(FP4X4), w_planes[0][:, cols]
            if proj == 1:
                return wk_sb[:, cols].bitcast(FP8X4), w_planes[1][PLANE_ROW[1]:P, cols]
            return wv_codes[:, cols].bitcast(FP8X4), wv_scales[:, cols]

        def product(proj, tt, nh, dst, copy):
            tokens = slice(tt * P, (tt + 1) * P)
            rhs, rhs_scale = weights(proj, nh)
            acc = psum.tile([P, N_TILE], F32, name="acc")
            nc.tensor.matmul_mx(out=acc[:], lhsT=x_codes[proj][:, tokens].bitcast(FP8X4), lhsT_scale=x_scales[proj][:, tokens],
                                rhs=rhs, rhs_scale=rhs_scale, start=True, stop=True)
            copy(out=dst, in_=acc[:])

        def full_rows(proj, out, tt, copies):
            res = results.tile([P, 2, N_TILE], F32, name="res")
            for nh in range(2):
                product(proj, tt, nh, res[:, nh, :], copies[nh])
            nc.sync.dma_start(out=out[tt * P:(tt + 1) * P, :], in_=res[:].rearrange("p a n -> p (a n)"))

        def subtract(j, cols):
            nc.vector.tensor_tensor(out=diff[:, j, cols], in0=before[:, j, cols], in1=now[:, j, cols], op=ALU.subtract)

        def scale_diff(step, proj, j, cols):
            nc.scalar.activation(out=step[:, j, cols], in_=diff[:, j, cols], func=ACT.Copy, scale=mu_col(j, proj))

        def cast_wv(nh):
            cols = slice(nh * N_TILE, (nh + 1) * N_TILE)
            nc.vector.tensor_copy(out=words_by_runs(wv16[:, cols, :]), in_=by_runs(wv_sb[:, :, cols]))

        def quantize_wv(nh):
            quantize(wv_codes, wv_scales, wv16, slice(nh * N_TILE, (nh + 1) * N_TILE))

        every = slice(0, T)
        scalar_only = [nc.scalar.copy, nc.scalar.copy]
        both = [nc.vector.tensor_copy, nc.scalar.copy]

        nc.vector.tensor_copy(out=mu_sb[:], in_=mu_raw[:])
        for h in range(2):
            subtract(0, halves(h))
            scale_diff(step_r, 0, 0, halves(h))
        scale_diff(step_k, 1, 0, every)
        blend_v_row(0, 0)
        for j in (1, 2):
            subtract(j, every)
            scale_diff(step_r, 0, j, every)
        subtract(3, halves(0))
        subtract(3, halves(1))
        for cols in (tile_cols(0), tile_cols(1), halves(1)):
            scale_diff(step_r, 0, 3, cols)
        for j in range(1, PACK):
            scale_diff(step_k, 1, j, every)

        blend_v_row(1, 0)
        add_step(0, step_r, tile_cols(0))
        add_step(0, step_r, tile_cols(1))
        quantize_x(0, tile_cols(0))
        add_step(0, step_r, tile_cols(2))
        quantize_x(0, tile_cols(1))
        add_step(0, step_r, tile_cols(3))
        blend_v_row(2, 0)
        quantize_x(0, halves(1))
        for tt in range(4):
            full_rows(0, out_0, tt, scalar_only)
        add_step(1, step_k, halves(0))
        add_step(1, step_k, halves(1))
        quantize_x(1, halves(0))
        blend_v_row(3, 0)
        quantize_x(1, halves(1))
        for tt in range(4):
            full_rows(1, out_1, tt, scalar_only)
        cast_wv(0)
        interleave_v(halves(0))
        quantize_wv(0)
        quantize_x(2, halves(0))
        cast_wv(1)
        blend_v_row(0, 1)
        quantize_wv(1)
        for j in range(1, PACK):
            blend_v_row(j, 1)
        interleave_v(tile_cols(2))
        interleave_v(tile_cols(3))
        quantize_x(2, tile_cols(2))
        quantize_x(2, tile_cols(3))
        for tt in range(4):
            full_rows(2, out_2, tt, scalar_only if tt < 2 else both)
